import numpy as np, ml_dtypes
CORES = [36,38,116,118,124,126,164,166,244,246,252,254]
N = 12
TOK, K, FT = 32, 3, 2
ROUTE = [[[6,7,8],[5,6,8],[1,7,8],[7,8,11],[0,5,9],[5,6,7],[3,9,11],[1,3,10],[1,4,11],[0,10,11],[3,6,8],[0,9,10],[2,8,11],[1,5,6],[0,7,10],[3,7,11],[5,6,10],[7,8,11],[4,5,8],[1,6,7],[0,3,9],[5,8,9],[1,7,11],[4,9,10],[2,7,9],[3,4,10],[2,6,8],[2,4,7],[2,4,7],[2,4,11],[0,5,9],[3,5,7]],[[3,4,11],[2,5,6],[2,9,10],[3,4,10],[2,5,9],[0,10,11],[6,7,11],[2,4,7],[6,7,10],[1,6,7],[4,8,10],[6,8,10],[2,3,5],[2,6,10],[5,7,11],[3,5,10],[0,5,11],[6,7,8],[1,5,9],[6,7,11],[8,9,10],[6,7,9],[3,6,9],[1,4,8],[0,4,10],[6,9,11],[1,3,6],[3,4,5],[2,3,10],[1,4,9],[2,5,8],[2,4,7]],[[5,9,11],[1,2,3],[0,3,11],[4,7,10],[1,7,9],[0,2,3],[2,8,9],[0,10,11],[0,8,11],[0,3,8],[2,8,11],[0,2,9],[0,3,7],[5,8,9],[5,7,11],[1,2,11],[3,7,9],[1,6,8],[0,1,2],[3,8,10],[4,8,9],[1,9,11],[2,5,10],[4,8,11],[4,5,10],[5,8,9],[1,8,10],[0,4,7],[6,7,9],[2,4,9],[0,1,10],[0,6,9]],[[3,6,10],[0,5,6],[5,8,9],[5,10,11],[4,9,10],[0,7,8],[0,7,10],[1,4,5],[9,10,11],[1,5,6],[0,4,5],[0,3,5],[2,4,6],[0,3,7],[2,6,11],[1,7,9],[0,2,11],[5,8,11],[2,6,10],[1,2,9],[0,2,4],[6,7,11],[4,10,11],[3,4,6],[0,5,11],[1,8,9],[1,4,9],[1,8,9],[6,8,10],[5,7,8],[4,5,8],[1,4,8]],[[1,6,11],[1,2,6],[0,2,5],[0,1,3],[0,3,7],[3,8,10],[1,5,6],[2,9,11],[4,9,11],[1,3,8],[1,3,4],[1,7,10],[0,2,3],[0,5,9],[3,6,11],[1,2,7],[7,8,9],[1,2,6],[0,2,8],[2,3,6],[0,9,11],[7,9,10],[8,9,10],[0,2,4],[0,2,10],[2,5,9],[4,5,8],[5,7,10],[0,2,5],[1,2,6],[0,7,10],[7,9,10]],[[5,7,8],[0,6,11],[3,5,10],[4,6,9],[7,9,11],[0,3,9],[5,10,11],[3,4,9],[0,1,6],[0,6,7],[3,4,11],[4,7,10],[1,7,11],[4,8,9],[3,6,10],[0,6,11],[2,6,7],[0,1,2],[3,4,6],[4,7,9],[2,7,10],[3,6,11],[2,5,6],[2,4,7],[6,8,10],[3,5,6],[4,7,9],[0,3,8],[2,4,7],[1,2,7],[0,2,11],[4,5,7]],[[1,9,10],[3,4,9],[4,5,9],[2,5,8],[1,3,9],[6,7,10],[1,4,8],[0,3,11],[3,6,8],[1,7,8],[0,2,6],[7,8,11],[0,3,11],[1,7,9],[0,2,7],[5,9,11],[3,6,11],[0,3,8],[2,8,10],[2,6,8],[4,5,9],[6,9,11],[0,2,10],[1,3,11],[0,2,10],[1,3,11],[0,1,5],[5,7,10],[2,3,11],[3,4,10],[2,4,6],[0,10,11]],[[8,10,11],[1,3,4],[6,7,8],[2,4,8],[0,1,3],[1,4,9],[0,5,8],[6,10,11],[5,10,11],[3,5,11],[1,2,3],[8,9,10],[0,1,6],[0,1,11],[6,8,10],[0,2,4],[0,5,6],[1,4,5],[0,4,6],[3,6,7],[1,3,6],[0,3,6],[3,5,7],[0,1,7],[1,2,5],[5,7,8],[1,7,9],[1,4,9],[1,5,8],[0,4,10],[4,5,8],[7,9,10]],[[1,4,5],[2,3,10],[0,4,8],[1,4,11],[3,9,11],[2,3,9],[0,3,5],[0,1,11],[0,8,9],[4,7,9],[3,4,8],[1,5,6],[7,9,10],[1,4,10],[1,3,4],[4,5,7],[3,4,10],[2,8,11],[6,10,11],[0,6,11],[3,8,10],[2,3,10],[1,2,7],[0,2,7],[7,8,11],[0,2,6],[6,7,9],[1,3,5],[3,4,9],[4,5,11],[4,8,10],[5,6,11]],[[0,2,4],[4,5,10],[3,5,9],[2,7,11],[2,3,7],[1,4,6],[2,4,7],[0,1,5],[2,9,10],[2,7,9],[1,7,8],[1,10,11],[3,5,6],[0,7,10],[1,7,10],[2,6,10],[7,10,11],[0,8,11],[5,7,9],[4,7,11],[3,9,11],[2,5,10],[4,10,11],[1,6,9],[0,1,11],[1,5,11],[5,6,10],[2,4,7],[1,8,10],[1,2,3],[3,7,11],[2,8,9]],[[5,6,11],[0,6,11],[0,1,4],[0,3,6],[3,7,11],[2,10,11],[1,2,10],[0,2,7],[4,9,10],[2,3,11],[6,7,11],[1,6,9],[0,2,6],[1,5,7],[1,2,10],[1,2,6],[5,7,8],[1,4,9],[0,4,8],[2,3,9],[0,6,8],[1,7,10],[4,10,11],[3,5,10],[2,7,8],[8,9,10],[3,6,11],[0,2,9],[3,5,7],[6,7,11],[0,2,5],[2,5,11]],[[4,7,8],[0,5,11],[2,8,11],[3,9,11],[0,1,8],[1,7,11],[3,4,8],[0,2,6],[1,6,8],[1,5,6],[0,2,9],[5,10,11],[0,1,4],[1,5,11],[0,4,9],[1,7,9],[7,9,10],[6,9,11],[0,3,11],[2,4,9],[3,7,11],[0,3,10],[7,9,11],[4,5,9],[2,5,9],[0,4,10],[1,4,6],[6,8,10],[2,6,10],[3,6,9],[1,5,8],[3,4,7]]]
def setup_inputs(rng):
    return {"x": rng.standard_normal((N, 128, TOK), dtype=np.float32).astype(ml_dtypes.bfloat16), "gate": (0.5 * rng.integers(1, 4, size=(N, K, TOK)) * (2 * rng.integers(0, 2, size=(N, K, TOK)) - 1)).astype(np.float32).astype(ml_dtypes.bfloat16), "w1": (rng.standard_normal((N, 128, FT * 128), dtype=np.float32) / 8).astype(ml_dtypes.bfloat16), "w2": (rng.standard_normal((N, 128, FT * 128), dtype=np.float32) / 8).astype(ml_dtypes.bfloat16)}
def setup_inputs_big(rng):
    d = setup_inputs(rng)
    for k in ("x", "gate", "w1", "w2"): d[k] = (d[k].astype(np.float32) * 1024.0).astype(d[k].dtype)
    return d
def setup_inputs_small(rng):
    d = setup_inputs(rng)
    for k in ("x", "gate", "w1", "w2"): d[k] = (d[k].astype(np.float32) * (1 / 1024.0)).astype(d[k].dtype)
    return d
def reference(x, gate, w1, w2):
    X, GATE, W1, W2 = x.astype(np.float64), gate.astype(np.float64), w1.astype(np.float64), w2.astype(np.float64)
    y = np.zeros((N, 128, TOK))
    for r in range(N):
        for t in range(TOK):
            for i, e in enumerate(ROUTE[r][t]):
                hid = np.maximum(W1[e].T @ X[r][:, t], 0.0)
                y[r][:, t] += GATE[r][i, t] * sum(W2[e][:, 128 * f:128 * f + 128].T @ hid[128 * f:128 * f + 128] for f in range(FT))
    return {"y": y.astype(ml_dtypes.bfloat16)}

from concourse.bass import DstId, RemoteDMATransfer
from concourse.mybir import AluOpType

SCRATCH = {
    "xin": ("sbuf", [128, 192], "bfloat16"),
    "wt": ("sbuf", [128, 2, 512], "bfloat16"),
    "zero": ("sbuf", [128, 64], "float32"),
    "hid": ("sbuf", [128, 8, 64], "bfloat16"),
    "ret": ("sbuf", [128, 4, 2, 32], "bfloat16"),
    "land": ("sbuf", [128, 384], "bfloat16"),
    "grow": ("sbuf", [128, 96], "bfloat16"),
    "ones": ("sbuf", [128, 128], "bfloat16"),
    "prod": ("sbuf", [128, 384], "float32"),
    "accs": ("sbuf", [128, 64], "float32"),
    "yb": ("sbuf", [128, 32], "bfloat16"),
    "p1_0": ("psum", [128, 512], "float32"),
    "p1_1": ("psum", [128, 512], "float32"),
    "p1_2": ("psum", [128, 512], "float32"),
    "p1_3": ("psum", [128, 512], "float32"),
    "p2_0": ("psum", [128, 512], "float32"),
    "p2_1": ("psum", [128, 512], "float32"),
    "gf": ("psum", [128, 512], "float32"),
    "acc": ("psum", [128, 512], "float32"),
}
SEMAPHORES = (["sx", "sxs", "swl", "swr", "sgl", "sz", "sg", "sv", "sy", "loc"]
              + ["xc%d" % c for c in range(6)]
              + ["sl%d" % c for c in range(6)]
              + ["m1_%d_%d" % (q, k) for q in range(2) for k in range(4)]
              + ["rl_%d_%d" % (q, k) for q in range(2) for k in range(4)]
              + ["m2_%d_%d" % (q, a) for q in range(2) for a in range(2)]
              + ["cp_%d_%d" % (q, a) for q in range(2) for a in range(2)])
_CACHE = {}


def _bits(m):
    return [b for b in range(m.bit_length()) if (m >> b) & 1]


def _mk(bl):
    return sum(1 << b for b in bl)


def _split(bl, k):
    per = 1
    while per * 2 * k <= len(bl):
        per *= 2
    return [bl[i * per:(i + 1) * per] for i in range(k)]


def _best_split(items, ws, ok, due):
    best = [None, None]

    def end(ps):
        d = sorted(due(p) for p in ps)
        return max(d[0] + 2, d[1]) + 2

    def rec(i, got):
        if i == len(items):
            ends = [end(got[w]) for w in ws]
            key = (max(ends), sum(ends))
            if best[0] is None or key < best[0]:
                best[0], best[1] = key, {p: w for w in ws for p in got[w]}
            return
        for w in ws:
            if len(got[w]) < 2 and ok(w, items[i]):
                got[w].append(items[i])
                rec(i + 1, got)
                got[w].pop()

    rec(0, {w: [] for w in ws})
    return best[1]


def _plan(T, topo):
    if "P" in _CACHE:
        return _CACHE["P"]
    cores = list(T.cores)
    place = lambda k: (topo.host(k), topo.chip(k))
    keys = []
    for k in cores:
        if place(k) not in keys:
            keys.append(place(k))
    ranks_on = [[k for k in cores if place(k) == key] for key in keys]
    nsim = (max(topo.host(k) for k in cores) + 1) * topo.CORES_PER_HOST
    nchip = len(keys)
    helper, workers = [], []
    for c in range(nchip):
        r0 = ranks_on[c][0]
        h = [k for k in range(nsim) if place(k) == keys[c] and k not in cores and topo.die(k) == topo.die(r0)
             and all(topo.may_write(k, d) for d in cores)][0]
        helper.append(h)
        workers.append(ranks_on[c] + [h])
    reach = lambda w, p: all(topo.may_write(w, d) for d in workers[p])
    sender, sends = [], {}
    for c in range(nchip):
        ws = workers[c]
        load = {w: (1.5 if w == helper[c] else 0) for w in ws}
        turn = [(c + k) % nchip for k in range(1, nchip)]
        able = {p: [w for w in ws if reach(w, p)] for p in turn}
        sd = {}
        for p in sorted(turn, key=lambda p: len(able[p])):
            w = min(able[p], key=lambda w: (load[w], ws.index(w)))
            sd[p] = w
            load[w] += 1
            sends.setdefault(w, []).append(p)
        sender.append(sd)
    due = lambda c, p: 0 if p == c else (2.5 if sender[p][c] == helper[p] else 1 + sends[sender[p][c]].index(c))
    handle = [_best_split(list(range(nchip)), workers[c], lambda w, p: p == c or reach(w, p), lambda p: due(c, p))
              for c in range(nchip)]
    order, slot = {}, {}
    for c in range(nchip):
        for w in workers[c]:
            mine = [p for p in range(nchip) if handle[c][p] == w]
            mine.sort(key=lambda p: due(c, p))
            order[w] = mine
            n = 1
            for p in mine:
                if p == c:
                    slot[(w, p)] = 0
                else:
                    slot[(w, p)] = n
                    n += 1
    chip_of = {w: c for c in range(nchip) for w in workers[c]}
    _CACHE["P"] = dict(cores=cores, ranks_on=ranks_on, helper=helper, workers=workers, handle=handle, order=order, slot=slot,
                       chip_of=chip_of, nchip=nchip, sender=sender, sends=sends, due=due)
    return _CACHE["P"]


def _engines(P, topo, w):
    c = P["chip_of"][w]
    far = [d for d in P["cores"] if P["chip_of"][d] != c and topo.may_write(w, d)][0]
    near = [d for d in P["workers"][c] if d != w][0]
    lo = _bits(topo.mask(w, far))
    return lo, [b for b in _bits(topo.mask(w, near)) if b not in lo]


def _ret_masks(P, topo, w, p):
    lo, hi = _engines(P, topo, w)
    homes = [d for d in P["ranks_on"][p] if d != w]
    parts = _split(hi if p == P["chip_of"][w] and w in P["cores"] else lo, len(homes))
    return {d: parts[i] for i, d in enumerate(homes)}


def _gate_groups(pts):
    left = set(pts)
    out = []
    while left:
        srt = sorted(left)
        best = (1, srt[0], (1, 1))
        for i, p in enumerate(srt):
            for q in srt[i + 1:]:
                dk, dd = q[0] - p[0], q[1] - p[1]
                if dk <= 0 or dd <= 0:
                    continue
                m = 2
                while (p[0] + m * dk, p[1] + m * dd) in left:
                    m += 1
                if m > best[0]:
                    best = (m, p, (dk, dd))
        m, p, (dk, dd) = best
        for j in range(m):
            left.remove((p[0] + j * dk, p[1] + j * dd))
        out.append((m, p[0], dk, p[1], dd))
    return out


def rank_program(g, core, T, topo):
    P = _plan(T, topo)
    if core not in P["chip_of"]:
        return
    S = T.sem
    c = P["chip_of"][core]
    rank = T.rank_of(core)
    ranks_on, handle, order, slot = P["ranks_on"], P["handle"], P["order"], P["slot"]
    mates_on_chip = [w for w in P["workers"][c] if w != core]
    lo, hi = _engines(P, topo, core)
    nlo = len(lo)
    TOK = T.tables["TOK"]
    BLK = 2 * TOK
    loc = [0]

    def dst(d):
        rid, pid = topo.addr(d, core)
        return DstId(rid=rid, pnc=pid)

    def fused(trs, n):
        g.remote_dma_fused(trs, local_sem=S.loc)
        loc[0] += n

    nz = 1
    g.vector.memset(T.zero[:, :], 0.0).then_inc(S.sz, 1)
    if rank is not None:
        a_me = ranks_on[c].index(core)
        g.sync.dma_start(T.xin[:, a_me * TOK:(a_me + 1) * TOK], T.x[:, :]).then_inc(S.sx, 16)
        g.scalar.dma_start(T.grow[0:1, :], T.gate[:, :]).then_inc(S.sgl, 16)
        g.sync.dma_start(T.wt[:, a_me, 0:256], T.w1[:, :]).then_inc(S.swl, 16)
        g.scalar.dma_start(T.wt[:, a_me, 256:512], T.w2[:, :]).then_inc(S.swl, 16)
        g.vector.memset(T.ones[0:1, :], 1.0).then_inc(S.sz, 1)
        g.vector.memset(T.gf[:, 0:P["nchip"] * BLK], 0.0).then_inc(S.sz, 1)
        nz = 3
    g.vector.wait_ge(S.sz, nz)

    if rank is not None:
        g.wait_ge(S.sx, 16)
        mine = T.xin[:, a_me * TOK:(a_me + 1) * TOK]
        fused([RemoteDMATransfer(dst_ids=[dst(d) for d in mates_on_chip], dma_engine_mask=_mk(lo), remote_sem=S.sxs,
                                 srcs=[mine], dsts=[mine for d in mates_on_chip], alu_op=0)], nlo)
        g.wait_ge(S.swl, 32)
        wm = T.wt[:, a_me, :]
        fused([RemoteDMATransfer(dst_ids=[dst(d) for d in mates_on_chip], dma_engine_mask=_mk(hi), remote_sem=S.swr,
                                 srcs=[wm], dsts=[wm for d in mates_on_chip], alu_op=0)], len(hi))
    n_sxs = nlo * (1 if rank is not None else 2)
    n_swr = len(hi) * (1 if rank is not None else 2)
    g.wait_ge(S.sxs, n_sxs)
    to = P["sends"].get(core, [])
    if to:
        fused([RemoteDMATransfer(dst_ids=[dst(handle[p][c]) for p in to], dma_engine_mask=_mk(lo), remote_sem=S["xc%d" % c],
                                 srcs=[T.xin[:, 0:BLK]],
                                 dsts=[T.xin[:, slot[(handle[p][c], c)] * BLK:(slot[(handle[p][c], c)] + 1) * BLK] for p in to],
                                 alu_op=0)], nlo)

    if rank is not None:
        route = T.tables["ROUTE"][rank]
        col = {}
        for p in range(P["nchip"]):
            for a, d in enumerate(ranks_on[p]):
                col[T.rank_of(d)] = (2 * p + a) * TOK
        pts = [(i * TOK + t, col[e] + t) for t in range(TOK) for i, e in enumerate(route[t])]
        groups = _gate_groups(pts)
        g.tensor.wait_ge(S.sz, nz)
        g.tensor.wait_ge(S.sgl, 16)
        for (m, k0, dk, d0, dd) in groups:
            g.tensor.matmul(T.gf[:, d0:d0 + (m - 1) * dd + 1:dd], T.ones[0:1, :], T.grow[0:1, k0:k0 + (m - 1) * dk + 1:dk],
                            True, True).then_inc(S.sg, 1)

    p1 = [T.p1_0, T.p1_1, T.p1_2, T.p1_3]
    p2 = [T.p2_0, T.p2_1]
    if rank is not None:
        g.tensor.wait_ge(S.swl, 32)
    g.tensor.wait_ge(S.swr, n_swr)
    for q, p in enumerate(order[core]):
        s = slot[(core, p)]
        if p == c:
            if rank is not None:
                g.tensor.wait_ge(S.sx, 16)
            g.tensor.wait_ge(S.sxs, n_sxs)
        else:
            g.tensor.wait_ge(S["xc%d" % p], len(_engines(P, topo, P["sender"][p][c])[0]))
        rhs = T.xin[:, s * BLK:(s + 1) * BLK]
        for k in range(4):
            a, f = k // 2, k % 2
            g.tensor.matmul(p1[k][:, 0:BLK], T.wt[:, a, 128 * f:128 * f + 128], rhs, True, True).then_inc(S["m1_%d_%d" % (q, k)], 1)
            g.vector.wait_ge(S["m1_%d_%d" % (q, k)], 1)
            g.vector.tensor_tensor(T.hid[:, 4 * q + k, :], p1[k][:, 0:BLK], T.zero[:, :], AluOpType.max).then_inc(S["rl_%d_%d" % (q, k)], 1)
        for a in range(2):
            if q > 0:
                g.tensor.wait_ge(S["cp_%d_%d" % (q - 1, a)], 1)
            for f in range(2):
                k = 2 * a + f
                g.tensor.wait_ge(S["rl_%d_%d" % (q, k)], 1)
                g.tensor.matmul(p2[a][:, 0:BLK], T.wt[:, a, 256 + 128 * f:256 + 128 * f + 128], T.hid[:, 4 * q + k, :],
                                f == 0, f == 1).then_inc(S["m2_%d_%d" % (q, a)], 1)
            g.vector.wait_ge(S["m2_%d_%d" % (q, a)], 2)
            g.vector.tensor_copy(T.ret[:, 2 * q:2 * q + 2, a, :], p2[a][:, 0:BLK]).then_inc(S["cp_%d_%d" % (q, a)], 1)
        g.wait_ge(S["cp_%d_%d" % (q, 0)], 1)
        g.wait_ge(S["cp_%d_%d" % (q, 1)], 1)
        masks = _ret_masks(P, topo, core, p)
        trs = [RemoteDMATransfer(dst_ids=[dst(d)], dma_engine_mask=_mk(masks[d]), remote_sem=S["sl%d" % c],
                                 src=T.ret[:, 2 * q + j], dst=T.land[:, c * BLK:(c + 1) * BLK], alu_op=0)
               for j, d in enumerate(ranks_on[p]) if d != core]
        fused(trs, sum(len(masks[d]) for d in masks))

    if rank is not None:
        def late(p):
            return (-1, 0) if p == c else (order[handle[p][c]].index(c), P["due"](p, c))
        blocks = sorted(range(P["nchip"]), key=late)
        g.vector.wait_ge(S.sg, len(groups))
        cnt = 0
        for b, p in enumerate(blocks):
            w = handle[p][c]
            if w == core:
                q = order[core].index(c)
                g.vector.wait_ge(S["cp_%d_%d" % (q, 0)], 1)
                g.vector.wait_ge(S["cp_%d_%d" % (q, 1)], 1)
                src = T.ret[:, 2 * q + a_me]
            else:
                g.vector.wait_ge(S["sl%d" % p], len(_ret_masks(P, topo, w, c)[core]))
                src = T.land[:, p * BLK:(p + 1) * BLK]
            gfb = T.gf[:, p * BLK:(p + 1) * BLK]
            if b == 0:
                g.vector.tensor_tensor(T.acc[:, 0:BLK], src, gfb, AluOpType.mult).then_inc(S.sv, 1)
                cnt += 1
                continue
            pr = T.prod[:, b * BLK:(b + 1) * BLK]
            g.vector.tensor_tensor(pr, src, gfb, AluOpType.mult).then_inc(S.sv, 1)
            cnt += 1
            g.vector.wait_ge(S.sv, cnt)
            out = T.accs[:, :] if b == len(blocks) - 1 else T.acc[:, 0:BLK]
            g.vector.tensor_tensor(out, T.acc[:, 0:BLK], pr, AluOpType.add).then_inc(S.sv, 1)
            cnt += 1
        g.vector.wait_ge(S.sv, cnt)
        g.vector.tensor_tensor(T.yb[:, :], T.accs[:, 0:TOK], T.accs[:, TOK:BLK], AluOpType.add).then_inc(S.sv, 1)
        cnt += 1
        g.sync.wait_ge(S.sv, cnt)
        g.sync.dma_start(T.y[:, :], T.yb[:, :]).then_inc(S.sy, 16)
        g.sync.wait_ge(S.sy, 16)
    g.wait_ge(S.loc, loc[0])
